import numpy as np
import ml_dtypes


def mxq(x, axis, fmt="e4m3"):
    dtype, down = {"e4m3": (ml_dtypes.float8_e4m3fn, 7), "e5m2": (ml_dtypes.float8_e5m2, 14)}[fmt]
    v = np.moveaxis(np.asarray(x, np.float32).astype(ml_dtypes.bfloat16).astype(np.float64), axis, -1)
    blocks = v.reshape(v.shape[:-1] + (-1, 32))
    amax = np.abs(blocks).max(-1, keepdims=True)
    byte = np.maximum(np.where(amax > 0, np.frexp(amax)[1] - 1 + 127, 0) - down, 1)
    scale = np.exp2(byte - 127.0)
    codes = (blocks / scale).astype(np.float32).astype(dtype).astype(np.float64)
    return np.moveaxis((codes * scale).reshape(v.shape), -1, axis)


WIDE = False


def mx_kscale(k):
    if not WIDE:
        return np.ones(k)
    levels = np.array([10, -10, 5, -5, 0])
    if k % 512:
        return np.exp2(np.random.permutation(np.resize(levels, k // 32))).repeat(32)
    a = np.empty((k // 512, 16))
    for p in range(k // 512):
        a[p, :8] = np.random.permutation(np.resize(levels, 8))
        for g in range(8):
            far = levels[np.abs(levels - a[p, g]) >= 10]
            a[p, g + 8] = far[np.random.randint(len(far))]
    return np.exp2(a.ravel()).repeat(32)


BF16 = ml_dtypes.bfloat16


def bf(x):
    return np.asarray(x, np.float32).astype(BF16)


def f64(x):
    return np.asarray(x).astype(np.float64)


E2M1 = np.array([0.0, 0.5, 1.0, 1.5, 2.0, 3.0, 4.0, 6.0, -0.0, -0.5, -1.0, -1.5, -2.0, -3.0, -4.0, -6.0])


def pack_weight(w, fmt):
    k, n = w.shape
    w = f64(bf(w)).reshape(k // 32, 32, n)
    amax = np.abs(w).max(1)
    if fmt == "e4m3":
        byte = np.frexp(amax)[1] - 1 + 127 - 7
    else:
        mant, ex = np.frexp(amax / 6.0)
        byte = np.where(mant > 0.5, ex, ex - 1) + 127
    byte = np.clip(np.where(amax > 0, byte, 1), 1, 254)
    scaled = (w * np.exp2(127.0 - byte)[:, None, :]).reshape(k, n).astype(np.float32)
    by_word = np.ascontiguousarray(scaled.reshape(k // 512, 128, 4, n).transpose(0, 1, 3, 2))
    if fmt == "e4m3":
        words = by_word.astype(ml_dtypes.float8_e4m3fn).view(np.uint8)
    else:
        c = by_word.astype(ml_dtypes.float4_e2m1fn).view(np.uint8) & 0xF
        words = c[..., 0::2] | (c[..., 1::2] << 4)
    return np.ascontiguousarray(words), np.ascontiguousarray(byte.astype(np.uint8).reshape(k // 512, 16, n))


def unpack_weight(words, scales, fmt):
    g, p, n, _ = words.shape
    if fmt == "e4m3":
        vals = np.ascontiguousarray(words).view(ml_dtypes.float8_e4m3fn).astype(np.float64)
    else:
        nib = np.empty((g, p, n, 4), np.uint8)
        nib[..., 0::2] = words & 0xF
        nib[..., 1::2] = words >> 4
        vals = E2M1[nib]
    vals = vals * np.repeat(np.exp2(scales.astype(np.float64) - 127.0), 8, axis=1)[..., None]
    return vals.transpose(0, 1, 3, 2).reshape(g * 512, n)
def pack4(w):
    words, scales = pack_weight(w, "e2m1")
    return words.reshape(words.shape[0], 128, -1), scales


def unpack4(words, scales):
    return unpack_weight(words.reshape(words.shape[0], 128, -1, 2), scales, "e2m1")


M, KO, KR, N, F = 1024, 512, 1536, 2048, 1024

OUTLIER = 3.0


def setup_inputs():
    s = mx_kscale(KO)
    t = mx_kscale(KR)
    x_outlier = OUTLIER * np.random.standard_normal((M, KO)) * s
    x_rest = np.random.standard_normal((M, KR)) * t
    wo = np.random.standard_normal((KO, N)) / np.sqrt(KO + KR) / s[:, None]
    wr = np.random.standard_normal((KR, N)) / np.sqrt(KO + KR) / t[:, None]
    wo_words, wo_scales = pack_weight(wo, "e4m3")
    wr_words, wr_scales = pack4(wr)
    return {"x": bf(np.concatenate([x_outlier, x_rest], axis=1)),
            "wo_words": wo_words, "wo_scales": wo_scales,
            "wr_words": wr_words, "wr_scales": wr_scales,
            "bias": bf(0.3 * np.random.standard_normal(N))}


def reference(x, wo_words, wo_scales, wr_words, wr_scales, bias):
    x = f64(x)
    xo = mxq(x[:, :KO], 1, "e4m3")
    xr = mxq(x[:, KO:], 1, "e4m3")
    wo = unpack_weight(wo_words, wo_scales, "e4m3")
    wr = unpack4(wr_words, wr_scales)
    h = (xo @ wo) + (xr @ wr)
    h = h + f64(bias)
    gate, up = h[:, :F], h[:, F:]
    return gate / (1.0 + np.exp(-gate)) * up

@@ -1,0 +1,252 @@
+from contextlib import ExitStack
+
+import concourse.mybir as mybir
+from concourse.masks import make_identity
+
+M, K, N, F = 1024, 2048, 2048, 1024
+FLOPS = 2 * M * K * N
+
+F32 = mybir.dt.float32
+BF16 = mybir.dt.bfloat16
+I32 = mybir.dt.int32
+U32 = mybir.dt.uint32
+U8 = mybir.dt.uint8
+FP8X4 = mybir.dt.float8_e4m3fn_x4
+FP4X4 = mybir.dt.float4_e2m1fn_x4
+ADD = mybir.AluOpType.add
+MULT = mybir.AluOpType.mult
+SILU = mybir.ActivationFunctionType.Silu
+
+P = 128
+K_PASS = 512
+COLS = 512
+TILES = M // P
+GATE, UP = 0, 1
+PASS_PAIRS = ((1, 2), (3, 0))
+PAIR_WORDS = K_PASS // 2
+LEAD = 6
+DIRECT_TILES = 2
+VECTOR_SORT_TILES = 4
+
+
+def group_order():
+    order = []
+    gates = 0
+    ups = 0
+    total = 2 * TILES
+    while gates < LEAD:
+        order.append((GATE, gates))
+        gates = gates + 1
+    while ups < total:
+        order.append((UP, ups))
+        ups = ups + 1
+        if gates - ups > 1 and ups < total:
+            order.append((UP, ups))
+            ups = ups + 1
+        if gates < total:
+            order.append((GATE, gates))
+            gates = gates + 1
+    return order
+
+
+def tile_outlier_split_swiglu_s1_kernel(tc, x, wo_words, wo_scales, wr_words, wr_scales, bias, out):
+    nc = tc.nc
+    with ExitStack() as ctx:
+        keep = ctx.enter_context(tc.tile_pool(name="keep", bufs=1))
+        work = ctx.enter_context(tc.tile_pool(name="work", bufs=3))
+        psum = ctx.enter_context(tc.psum_pool(name="psum", bufs=4))
+        ctx.enter_context(tc.manual_schedule())
+
+        ident = keep.tile([P, P], F32, name="ident")
+        make_identity(nc, ident[:])
+
+        fp4_planes = []
+        for half in (GATE, UP):
+            plane = keep.tile([P, 3, F], U8, name="fp4_plane%d" % half, align_bytes=64)
+            fp4_planes.append(plane)
+        fp8_plane = keep.tile([P, N], U8, name="fp8_plane", align_bytes=64)
+        nc.vector.memset(fp4_planes[GATE][:].bitcast(I32), 0)
+        nc.vector.memset(fp8_plane[:].bitcast(I32), 0)
+        nc.vector.memset(fp4_planes[UP][:].bitcast(I32), 0)
+
+        fp4_scale_rows = wr_scales.bitcast(I32).rearrange("g (q r) w -> r q g w", r=4)
+        fp8_scale_rows = wo_scales[0].bitcast(I32).rearrange("(q r) w -> r q w", r=4)
+        fp4_rows = wr_words.bitcast(I32).rearrange("g p w -> p g w")
+        fp8_rows = wo_words[0].rearrange("p n t -> p (n t)").bitcast(I32)
+
+        def load_fp4_scales(half):
+            for r in range(4):
+                nc.sync.dma_start(
+                    out=fp4_planes[half][:].bitcast(I32)[r:P:32, :, :],
+                    in_=fp4_scale_rows[r][:, :, half * (F // 4) : (half + 1) * (F // 4)],
+                )
+
+        def load_fp8_scales():
+            for r in range(4):
+                nc.sync.dma_start(out=fp8_plane[:].bitcast(I32)[r:P:32, :], in_=fp8_scale_rows[r])
+
+        fp4_codes = {}
+        fp8_codes = {}
+
+        def load_weights(half, j):
+            col = half * F + j * COLS
+            c4 = keep.tile([P, 3, 2 * COLS], U8, name="fp4_codes%d%d" % (half, j), align_bytes=64)
+            nc.sync.dma_start(out=c4[:].bitcast(I32), in_=fp4_rows[:, :, col // 2 : (col + COLS) // 2])
+            c8 = keep.tile([P, 4 * COLS], U8, name="fp8_codes%d%d" % (half, j), align_bytes=64)
+            nc.sync.dma_start(out=c8[:].bitcast(I32), in_=fp8_rows[:, col : col + COLS])
+            fp4_codes[(half, j)] = c4
+            fp8_codes[(half, j)] = c8
+
+        x_words = {}
+        x_tiles = {}
+
+        def load_x(i):
+            t = keep.tile([P, K], BF16, name="x%d" % i, align_bytes=64)
+            nc.sync.dma_start(out=t[:], in_=x[i * P : (i + 1) * P, :])
+            x_tiles[i] = t
+            for g in range(4):
+                x_words[(i, g)] = t[:].bitcast(F32)[:, g * PAIR_WORDS : (g + 1) * PAIR_WORDS]
+
+        x0_first = keep.tile([P, 2 * K_PASS], BF16, name="x0_first", align_bytes=64)
+        x0_second = keep.tile([P, 2, K_PASS], BF16, name="x0_second", align_bytes=64)
+        nc.sync.dma_start(out=x0_first[:], in_=x[0:P, K_PASS : 3 * K_PASS])
+        nc.sync.dma_start(out=x0_second[:], in_=x[0:P, :].rearrange("m (g k) -> m g k", k=K_PASS)[:, 0:4:3, :])
+        x_words[(0, 1)] = x0_first[:].bitcast(F32)[:, 0:PAIR_WORDS]
+        x_words[(0, 2)] = x0_first[:].bitcast(F32)[:, PAIR_WORDS : 2 * PAIR_WORDS]
+        x_words[(0, 0)] = x0_second[:, 0, :].bitcast(F32)
+        x_words[(0, 3)] = x0_second[:, 1, :].bitcast(F32)
+
+        bias_cols = keep.tile([P, 2, 8], BF16, name="bias_cols", align_bytes=64)
+        nc.sync.dma_start(out=bias_cols[:], in_=bias.rearrange("(h p c) -> p h c", h=2, p=P))
+
+        load_fp4_scales(GATE)
+        load_weights(GATE, 0)
+        load_fp8_scales()
+        load_x(1)
+        load_weights(GATE, 1)
+        load_x(2)
+        load_x(3)
+        load_fp4_scales(UP)
+        load_weights(UP, 0)
+        load_weights(UP, 1)
+        for i in range(4, TILES):
+            load_x(i)
+
+        bias_rows = {}
+
+        def spread_bias(half):
+            bank = psum.tile([P, 4, P], F32, tag="turn", name="bias_bank")
+            for c in range(4):
+                nc.tensor.transpose(
+                    bank[:, c, :], bias_cols[:, half, :].bitcast(F32)[:, c : c + 1].to_broadcast([P, P]), ident[:]
+                )
+            row = keep.tile([P, F], BF16, name="bias_row%d" % half, align_bytes=64)
+            nc.scalar.copy(
+                out=row[:].bitcast(F32).rearrange("p (k c) -> p k c", c=4),
+                in_=bank[:].rearrange("p c k -> p k c"),
+            )
+            bias_rows[half] = row
+
+        sorted_words = {}
+
+        def sort_words(i):
+            t = work.tile([P, 4, 2, P], F32, tag="sorted", name="sorted", bufs=2, align_bytes=64)
+            src = x_tiles[i][:].bitcast(F32).rearrange("m (g p u) -> m g u p", g=4, u=2)
+            if i < VECTOR_SORT_TILES:
+                nc.vector.tensor_copy(out=t[:], in_=src)
+            else:
+                nc.scalar.copy(out=t[:], in_=src)
+            sorted_words[i] = t
+
+        x_codes = {}
+        x_scales = {}
+
+        def turn_pair(i, pair):
+            bank = psum.tile([P, 2, 2, P], F32, tag="turn", name="turn_bank")
+            for a, g in enumerate(PASS_PAIRS[pair]):
+                for u in range(2):
+                    if i < DIRECT_TILES:
+                        src = x_words[(i, g)][:, u:PAIR_WORDS:2]
+                    else:
+                        src = sorted_words[i][:, g, u, :]
+                    nc.tensor.transpose(bank[:, a, u, :], src, ident[:])
+            grouped = work.tile([P, 2 * 4 * P], BF16, tag="grouped", name="grouped", bufs=4, align_bytes=64)
+            nc.scalar.copy(
+                out=grouped[:].bitcast(F32).rearrange("p (a m u) -> p a m u", a=2, u=2),
+                in_=bank[:].rearrange("p a u m -> p a m u"),
+            )
+            return grouped
+
+        def quantize_pair(i, pair, grouped):
+            codes = keep.tile([P, 2 * P], U32, name="x_codes%d_%d" % (i, pair), align_bytes=64)
+            scales = keep.tile([P, 2 * P], U8, name="x_scales%d_%d" % (i, pair), align_bytes=64)
+            nc.vector.quantize_mx(out=codes[:].bitcast(FP8X4), scales=scales[:], in_=grouped[:])
+            for a, g in enumerate(PASS_PAIRS[pair]):
+                x_codes[(i, g)] = codes[:, a * P : (a + 1) * P]
+                x_scales[(i, g)] = scales[:, a * P : (a + 1) * P]
+
+        def prepare_tile(i):
+            turned = [turn_pair(i, pair) for pair in range(2)]
+            for pair in range(2):
+                quantize_pair(i, pair, turned[pair])
+
+        def multiply(half, n):
+            i, j = divmod(n, 2)
+            acc = psum.tile([P, COLS], F32, tag="acc", name="acc")
+            passes = PASS_PAIRS[0] + PASS_PAIRS[1]
+            for step, g in enumerate(passes):
+                if g == 0:
+                    rhs = fp8_codes[(half, j)][:].bitcast(FP8X4)
+                    col = half * F + j * COLS
+                    rhs_scale = fp8_plane[:, col : col + COLS]
+                else:
+                    rhs = fp4_codes[(half, j)][:, g - 1, :].bitcast(FP4X4)
+                    rhs_scale = fp4_planes[half][:, g - 1, j * COLS : (j + 1) * COLS]
+                nc.tensor.matmul_mx(
+                    out=acc[:],
+                    lhsT=x_codes[(i, g)].bitcast(FP8X4),
+                    lhsT_scale=x_scales[(i, g)],
+                    rhs=rhs,
+                    rhs_scale=rhs_scale,
+                    start=(step == 0),
+                    stop=(step == len(passes) - 1),
+                )
+            biased = work.tile([P, COLS], F32, tag="biased%d" % half, name="biased")
+            nc.vector.tensor_tensor(
+                out=biased[:], in0=acc[:], in1=bias_rows[half][:, j * COLS : (j + 1) * COLS], op=ADD
+            )
+            return biased
+
+        activated = {}
+
+        def activate(n, biased):
+            s = work.tile([P, COLS], F32, tag="silu", name="silu", bufs=LEAD + 3)
+            nc.scalar.activation(out=s[:], in_=biased[:], func=SILU)
+            activated[n] = s
+
+        def finish(n, biased):
+            i, j = divmod(n, 2)
+            result = keep.tile([P, COLS], F32, name="result%d" % n)
+            nc.vector.tensor_tensor(out=result[:], in0=biased[:], in1=activated[n][:], op=MULT)
+            nc.sync.dma_start(out=out[i * P : (i + 1) * P, j * COLS : (j + 1) * COLS], in_=result[:])
+
+        prepare_tile(0)
+        spread_bias(GATE)
+        waiting = None
+        for half, n in group_order():
+            biased = multiply(half, n)
+            if waiting is not None:
+                finish(*waiting)
+                waiting = None
+            if half == UP:
+                waiting = (n, biased)
+            else:
+                i, j = divmod(n, 2)
+                if n == 0:
+                    spread_bias(UP)
+                if j == 0 and i + 1 < TILES:
+                    prepare_tile(i + 1)
+                activate(n, biased)
+                if j == 1 and DIRECT_TILES <= i + 2 < TILES:
+                    sort_words(i + 2)
+        finish(*waiting)

@@ -18,33 +18,42 @@ MULT = mybir.AluOpType.mult
 SILU = mybir.ActivationFunctionType.Silu
 
 P = 128
-K_PASS = 512
 COLS = 512
+NARROW = 128
 TILES = M // P
 GATE, UP = 0, 1
 PASS_PAIRS = ((1, 2), (3, 0))
-PAIR_WORDS = K_PASS // 2
+PASS_ORDER = PASS_PAIRS[0] + PASS_PAIRS[1]
+FP8_PLANE_ROW = 4
 LEAD = 6
-DIRECT_TILES = 2
-VECTOR_SORT_TILES = 4
+MIN_LEAD = 0
+DIRECT_TILES = 0
+WARM_RUNS = (14, 8, 0, 0)
+TURN_AFTER = {(2, 0): [(3,)], (3, 1): [(4, 5)], (5, 1): [(6, 7)]}
+SORT_AFTER = {(2, 1): [4], (3, 0): [5], (4, 1): [6], (5, 0): [7]}
+TAIL_PIECES = [(0, 256), (256, 256)]
+
+
+def block_order():
+    blocks = [(0, 0), (1, 0), (0, 1), (1, 1)]
+    for i in range(2, TILES):
+        blocks.extend([(i, 0), (i, 1)])
+    return blocks
 
 
 def group_order():
-    order = []
-    gates = 0
+    blocks = block_order()
+    order = [(GATE, b) for b in blocks[:LEAD]]
+    gates = LEAD
     ups = 0
-    total = 2 * TILES
-    while gates < LEAD:
-        order.append((GATE, gates))
-        gates = gates + 1
-    while ups < total:
-        order.append((UP, ups))
+    while ups < len(blocks):
+        order.append((UP, blocks[ups]))
         ups = ups + 1
-        if gates - ups > 1 and ups < total:
-            order.append((UP, ups))
+        if gates - ups > MIN_LEAD and ups < len(blocks):
+            order.append((UP, blocks[ups]))
             ups = ups + 1
-        if gates < total:
-            order.append((GATE, gates))
+        if gates < len(blocks):
+            order.append((GATE, blocks[gates]))
             gates = gates + 1
     return order
 
@@ -57,33 +66,49 @@ def tile_outlier_split_swiglu_s1_kernel(tc, x, wo_words, wo_scales, wr_words, wr
         psum = ctx.enter_context(tc.psum_pool(name="psum", bufs=4))
         ctx.enter_context(tc.manual_schedule())
 
+        warm_in = keep.tile([P, 4 * P], BF16, name="warm_in", align_bytes=64)
+        warm_codes = keep.tile([P, P], U32, name="warm_codes", align_bytes=64)
+        warm_scales = keep.tile([P, P], U8, name="warm_scales", align_bytes=64)
+        warm_silu = keep.tile([P, 1], F32, name="warm_silu")
+        nc.vector.memset(warm_in[:], 1.0)
+        nc.scalar.activation(out=warm_silu[:], in_=warm_in[:, 0:1], func=SILU)
+
         ident = keep.tile([P, P], F32, name="ident")
         make_identity(nc, ident[:])
 
+        fp4_ranges = [(0, COLS), (COLS, COLS), (F, F)]
         fp4_planes = []
-        for half in (GATE, UP):
-            plane = keep.tile([P, 3, F], U8, name="fp4_plane%d" % half, align_bytes=64)
+        for start, width in fp4_ranges:
+            plane = keep.tile([P, 3, width], U8, name="fp4_plane%d" % start, align_bytes=64)
             fp4_planes.append(plane)
         fp8_plane = keep.tile([P, N], U8, name="fp8_plane", align_bytes=64)
-        nc.vector.memset(fp4_planes[GATE][:].bitcast(I32), 0)
+        nc.vector.memset(fp4_planes[0][:].bitcast(I32), 0)
+        nc.vector.quantize_mx(out=warm_codes[:].bitcast(FP8X4), scales=warm_scales[:], in_=warm_in[:])
         nc.vector.memset(fp8_plane[:].bitcast(I32), 0)
-        nc.vector.memset(fp4_planes[UP][:].bitcast(I32), 0)
+        nc.vector.memset(fp4_planes[1][:].bitcast(I32), 0)
+        nc.vector.memset(fp4_planes[2][:].bitcast(I32), 0)
 
         fp4_scale_rows = wr_scales.bitcast(I32).rearrange("g (q r) w -> r q g w", r=4)
         fp8_scale_rows = wo_scales[0].bitcast(I32).rearrange("(q r) w -> r q w", r=4)
         fp4_rows = wr_words.bitcast(I32).rearrange("g p w -> p g w")
         fp8_rows = wo_words[0].rearrange("p n t -> p (n t)").bitcast(I32)
 
-        def load_fp4_scales(half):
+        def load_fp4_scales(part):
+            start, width = fp4_ranges[part]
             for r in range(4):
                 nc.sync.dma_start(
-                    out=fp4_planes[half][:].bitcast(I32)[r:P:32, :, :],
-                    in_=fp4_scale_rows[r][:, :, half * (F // 4) : (half + 1) * (F // 4)],
+                    out=fp4_planes[part][:].bitcast(I32)[r:P:32, :, :],
+                    in_=fp4_scale_rows[r][:, :, start // 4 : (start + width) // 4],
                 )
+
+        def fp4_scales(g, col, width):
+            part = min(col // COLS, 2)
+            offset = col - fp4_ranges[part][0]
+            return fp4_planes[part][:, g - 1, offset : offset + width]
 
         def load_fp8_scales():
             for r in range(4):
-                nc.sync.dma_start(out=fp8_plane[:].bitcast(I32)[r:P:32, :], in_=fp8_scale_rows[r])
+                nc.sync.dma_start(out=fp8_plane[:].bitcast(I32)[FP8_PLANE_ROW + r : P : 32, :], in_=fp8_scale_rows[r])
 
         fp4_codes = {}
         fp8_codes = {}
@@ -97,49 +122,55 @@ def tile_outlier_split_swiglu_s1_kernel(tc, x, wo_words, wo_scales, wr_words, wr
             fp4_codes[(half, j)] = c4
             fp8_codes[(half, j)] = c8
 
-        x_words = {}
         x_tiles = {}
 
         def load_x(i):
             t = keep.tile([P, K], BF16, name="x%d" % i, align_bytes=64)
             nc.sync.dma_start(out=t[:], in_=x[i * P : (i + 1) * P, :])
             x_tiles[i] = t
-            for g in range(4):
-                x_words[(i, g)] = t[:].bitcast(F32)[:, g * PAIR_WORDS : (g + 1) * PAIR_WORDS]
 
-        x0_first = keep.tile([P, 2 * K_PASS], BF16, name="x0_first", align_bytes=64)
-        x0_second = keep.tile([P, 2, K_PASS], BF16, name="x0_second", align_bytes=64)
-        nc.sync.dma_start(out=x0_first[:], in_=x[0:P, K_PASS : 3 * K_PASS])
-        nc.sync.dma_start(out=x0_second[:], in_=x[0:P, :].rearrange("m (g k) -> m g k", k=K_PASS)[:, 0:4:3, :])
-        x_words[(0, 1)] = x0_first[:].bitcast(F32)[:, 0:PAIR_WORDS]
-        x_words[(0, 2)] = x0_first[:].bitcast(F32)[:, PAIR_WORDS : 2 * PAIR_WORDS]
-        x_words[(0, 0)] = x0_second[:, 0, :].bitcast(F32)
-        x_words[(0, 3)] = x0_second[:, 1, :].bitcast(F32)
-
+        load_x(0)
+        load_x(1)
         bias_cols = keep.tile([P, 2, 8], BF16, name="bias_cols", align_bytes=64)
         nc.sync.dma_start(out=bias_cols[:], in_=bias.rearrange("(h p c) -> p h c", h=2, p=P))
-
-        load_fp4_scales(GATE)
+        load_fp4_scales(0)
         load_weights(GATE, 0)
         load_fp8_scales()
-        load_x(1)
-        load_weights(GATE, 1)
         load_x(2)
+        load_fp4_scales(1)
+        load_weights(GATE, 1)
         load_x(3)
-        load_fp4_scales(UP)
+        load_fp4_scales(2)
         load_weights(UP, 0)
         load_weights(UP, 1)
         for i in range(4, TILES):
             load_x(i)
 
+        warm_bank = psum.tile([P, P], F32, tag="acc", name="warm_bank")
+
+        def warm(count):
+            for step in range(count):
+                nc.tensor.matmul_mx(
+                    out=warm_bank[:],
+                    lhsT=warm_codes[:].bitcast(FP8X4),
+                    lhsT_scale=warm_scales[:],
+                    rhs=warm_codes[:].bitcast(FP8X4),
+                    rhs_scale=warm_scales[:],
+                    start=True,
+                    stop=True,
+                )
+
         bias_rows = {}
 
-        def spread_bias(half):
+        def turn_bias(half):
             bank = psum.tile([P, 4, P], F32, tag="turn", name="bias_bank")
             for c in range(4):
                 nc.tensor.transpose(
                     bank[:, c, :], bias_cols[:, half, :].bitcast(F32)[:, c : c + 1].to_broadcast([P, P]), ident[:]
                 )
+            return bank
+
+        def copy_bias(half, bank):
             row = keep.tile([P, F], BF16, name="bias_row%d" % half, align_bytes=64)
             nc.scalar.copy(
                 out=row[:].bitcast(F32).rearrange("p (k c) -> p k c", c=4),
@@ -150,9 +181,9 @@ def tile_outlier_split_swiglu_s1_kernel(tc, x, wo_words, wo_scales, wr_words, wr
         sorted_words = {}
 
         def sort_words(i):
-            t = work.tile([P, 4, 2, P], F32, tag="sorted", name="sorted", bufs=2, align_bytes=64)
+            t = work.tile([P, 4, 2, P], F32, tag="sorted", name="sorted", bufs=3, align_bytes=64)
             src = x_tiles[i][:].bitcast(F32).rearrange("m (g p u) -> m g u p", g=4, u=2)
-            if i < VECTOR_SORT_TILES:
+            if i < 3:
                 nc.vector.tensor_copy(out=t[:], in_=src)
             else:
                 nc.scalar.copy(out=t[:], in_=src)
@@ -166,7 +197,7 @@ def tile_outlier_split_swiglu_s1_kernel(tc, x, wo_words, wo_scales, wr_words, wr
             for a, g in enumerate(PASS_PAIRS[pair]):
                 for u in range(2):
                     if i < DIRECT_TILES:
-                        src = x_words[(i, g)][:, u:PAIR_WORDS:2]
+                        src = x_tiles[i][:].bitcast(F32)[:, 2 * P * g + u : 2 * P * (g + 1) : 2]
                     else:
                         src = sorted_words[i][:, g, u, :]
                     nc.tensor.transpose(bank[:, a, u, :], src, ident[:])
@@ -190,63 +221,107 @@ def tile_outlier_split_swiglu_s1_kernel(tc, x, wo_words, wo_scales, wr_words, wr
             for pair in range(2):
                 quantize_pair(i, pair, turned[pair])
 
-        def multiply(half, n):
-            i, j = divmod(n, 2)
-            acc = psum.tile([P, COLS], F32, tag="acc", name="acc")
-            passes = PASS_PAIRS[0] + PASS_PAIRS[1]
-            for step, g in enumerate(passes):
-                if g == 0:
-                    rhs = fp8_codes[(half, j)][:].bitcast(FP8X4)
-                    col = half * F + j * COLS
-                    rhs_scale = fp8_plane[:, col : col + COLS]
-                else:
-                    rhs = fp4_codes[(half, j)][:, g - 1, :].bitcast(FP4X4)
-                    rhs_scale = fp4_planes[half][:, g - 1, j * COLS : (j + 1) * COLS]
-                nc.tensor.matmul_mx(
-                    out=acc[:],
-                    lhsT=x_codes[(i, g)].bitcast(FP8X4),
-                    lhsT_scale=x_scales[(i, g)],
-                    rhs=rhs,
-                    rhs_scale=rhs_scale,
-                    start=(step == 0),
-                    stop=(step == len(passes) - 1),
-                )
-            biased = work.tile([P, COLS], F32, tag="biased%d" % half, name="biased")
-            nc.vector.tensor_tensor(
-                out=biased[:], in0=acc[:], in1=bias_rows[half][:, j * COLS : (j + 1) * COLS], op=ADD
+        def mx_pass(acc, half, block, g, first, width):
+            i, j = block
+            col = half * F + j * COLS + first
+            if g == 0:
+                rhs = fp8_codes[(half, j)][:, 4 * first : 4 * (first + width)].bitcast(FP8X4)
+                rhs_scale = fp8_plane[FP8_PLANE_ROW:P, col : col + width]
+            else:
+                rhs = fp4_codes[(half, j)][:, g - 1, 2 * first : 2 * (first + width)].bitcast(FP4X4)
+                rhs_scale = fp4_scales(g, col, width)
+            nc.tensor.matmul_mx(
+                out=acc,
+                lhsT=x_codes[(i, g)].bitcast(FP8X4),
+                lhsT_scale=x_scales[(i, g)],
+                rhs=rhs,
+                rhs_scale=rhs_scale,
+                start=(g == PASS_ORDER[0]),
+                stop=(g == PASS_ORDER[-1]),
             )
+
+        def add_bias(acc, half, block, first, width):
+            biased = work.tile([P, COLS], F32, tag="biased%d" % half, name="biased", bufs=5)
+            col = block[1] * COLS + first
+            nc.vector.tensor_tensor(out=biased[:, 0:width], in0=acc, in1=bias_rows[half][:, col : col + width], op=ADD)
             return biased
 
         activated = {}
 
-        def activate(n, biased):
+        def activate(block, biased):
             s = work.tile([P, COLS], F32, tag="silu", name="silu", bufs=LEAD + 3)
             nc.scalar.activation(out=s[:], in_=biased[:], func=SILU)
-            activated[n] = s
+            activated[block] = s
 
-        def finish(n, biased):
-            i, j = divmod(n, 2)
-            result = keep.tile([P, COLS], F32, name="result%d" % n)
-            nc.vector.tensor_tensor(out=result[:], in0=biased[:], in1=activated[n][:], op=MULT)
-            nc.sync.dma_start(out=out[i * P : (i + 1) * P, j * COLS : (j + 1) * COLS], in_=result[:])
+        def finish(block, biased, first, width):
+            i, j = block
+            result = keep.tile([P, width], F32, name="result%d_%d_%d" % (i, j, first))
+            nc.vector.tensor_tensor(
+                out=result[:], in0=biased[:, 0:width], in1=activated[block][:, first : first + width], op=MULT
+            )
+            col = j * COLS + first
+            nc.sync.dma_start(out=out[i * P : (i + 1) * P, col : col + width], in_=result[:])
 
-        prepare_tile(0)
-        spread_bias(GATE)
+        order = group_order()
+
+        sort_words(0)
+        sort_words(1)
+        warm(WARM_RUNS[0])
+        turned = [turn_pair(0, pair) for pair in range(2)]
+        bias_banks = [turn_bias(half) for half in (GATE, UP)]
+        turned.extend([turn_pair(1, pair) for pair in range(2)])
+        for half in (GATE, UP):
+            copy_bias(half, bias_banks[half])
+        for n, grouped in enumerate(turned):
+            quantize_pair(n // 2, n % 2, grouped)
+        sort_words(2)
+
+        first_blocks = [order[0][1], order[1][1]]
+        first_accs = [psum.tile([P, COLS], F32, tag="acc", name="acc") for block in first_blocks]
+        for passes in (PASS_ORDER[:-1], PASS_ORDER[-1:]):
+            for acc, block in zip(first_accs, first_blocks):
+                for g in passes:
+                    mx_pass(acc[:], GATE, block, g, 0, COLS)
+        first_biased = [add_bias(acc[:], GATE, block, 0, COLS) for acc, block in zip(first_accs, first_blocks)]
+        prepare_tile(2)
+        for block, biased in zip(first_blocks, first_biased):
+            activate(block, biased)
+        sort_words(3)
+
         waiting = None
-        for half, n in group_order():
-            biased = multiply(half, n)
+        for half, block in order[2:-1]:
+            acc = psum.tile([P, COLS], F32, tag="acc", name="acc")
+            for g in PASS_ORDER:
+                mx_pass(acc[:], half, block, g, 0, COLS)
+            biased = add_bias(acc[:], half, block, 0, COLS)
             if waiting is not None:
                 finish(*waiting)
                 waiting = None
-            if half == UP:
-                waiting = (n, biased)
+            if half == UP and block == (TILES - 1, 0):
+                finish(block, biased, 0, COLS)
+            elif half == UP:
+                waiting = (block, biased, 0, COLS)
             else:
-                i, j = divmod(n, 2)
-                if n == 0:
-                    spread_bias(UP)
-                if j == 0 and i + 1 < TILES:
-                    prepare_tile(i + 1)
-                activate(n, biased)
-                if j == 1 and DIRECT_TILES <= i + 2 < TILES:
-                    sort_words(i + 2)
+                for tile in TURN_AFTER.get(block, ()):
+                    turned = [turn_pair(i, pair) for i in tile for pair in range(2)]
+                    for n, grouped in enumerate(turned):
+                        quantize_pair(tile[n // 2], n % 2, grouped)
+                activate(block, biased)
+                for i in SORT_AFTER.get(block, ()):
+                    sort_words(i)
+        if waiting is not None:
+            finish(*waiting)
+            waiting = None
+
+        block = order[-1][1]
+        for first, width in TAIL_PIECES:
+            acc = psum.tile([P, COLS], F32, tag="turn", name="tail_acc")
+            step = NARROW if width < COLS else COLS
+            for sub in range(0, width, step):
+                for g in PASS_ORDER:
+                    mx_pass(acc[:, sub : sub + step], UP, block, g, first + sub, step)
+            biased = add_bias(acc[:, 0:width], UP, block, first, width)
+            if waiting is not None:
+                finish(*waiting)
+            waiting = (block, biased, first, width)
         finish(*waiting)

@@ -22,13 +22,13 @@ COLS = 512
 NARROW = 128
 TILES = M // P
 GATE, UP = 0, 1
-PASS_PAIRS = ((1, 2), (3, 0))
-PASS_ORDER = PASS_PAIRS[0] + PASS_PAIRS[1]
+PASS_PAIRS = ((1, 2), (0, 3))
+PASS_ORDER = (1, 2, 3, 0)
 FP8_PLANE_ROW = 4
 LEAD = 6
 MIN_LEAD = 0
 DIRECT_TILES = 0
-WARM_RUNS = (14, 8, 0, 0)
+WARM_RUNS = (13, 8, 0, 0)
 TURN_AFTER = {(2, 0): [(3,)], (3, 1): [(4, 5)], (5, 1): [(6, 7)]}
 SORT_AFTER = {(2, 1): [4], (3, 0): [5], (4, 1): [6], (5, 0): [7]}
 TAIL_PIECES = [(0, 256), (256, 256)]
@@ -49,7 +49,7 @@ def group_order():
     while ups < len(blocks):
         order.append((UP, blocks[ups]))
         ups = ups + 1
-        if gates - ups > MIN_LEAD and ups < len(blocks):
+        if gates - ups > MIN_LEAD and ups < len(blocks) and (gates % 2 == 0 or gates - ups > len(blocks) - gates):
             order.append((UP, blocks[ups]))
             ups = ups + 1
         if gates < len(blocks):
@@ -81,22 +81,23 @@ def tile_outlier_split_swiglu_s1_kernel(tc, x, wo_words, wo_scales, wr_words, wr
         for start, width in fp4_ranges:
             plane = keep.tile([P, 3, width], U8, name="fp4_plane%d" % start, align_bytes=64)
             fp4_planes.append(plane)
-        fp8_plane = keep.tile([P, N], U8, name="fp8_plane", align_bytes=64)
+        fp8_planes = [keep.tile([P, F], U8, name="fp8_plane%d" % half, align_bytes=64) for half in (GATE, UP)]
         nc.vector.memset(fp4_planes[0][:].bitcast(I32), 0)
         nc.vector.quantize_mx(out=warm_codes[:].bitcast(FP8X4), scales=warm_scales[:], in_=warm_in[:])
-        nc.vector.memset(fp8_plane[:].bitcast(I32), 0)
+        nc.vector.memset(fp8_planes[GATE][:].bitcast(I32), 0)
         nc.vector.memset(fp4_planes[1][:].bitcast(I32), 0)
         nc.vector.memset(fp4_planes[2][:].bitcast(I32), 0)
+        nc.vector.memset(fp8_planes[UP][:].bitcast(I32), 0)
 
         fp4_scale_rows = wr_scales.bitcast(I32).rearrange("g (q r) w -> r q g w", r=4)
         fp8_scale_rows = wo_scales[0].bitcast(I32).rearrange("(q r) w -> r q w", r=4)
         fp4_rows = wr_words.bitcast(I32).rearrange("g p w -> p g w")
         fp8_rows = wo_words[0].rearrange("p n t -> p (n t)").bitcast(I32)
 
-        def load_fp4_scales(part):
+        def load_fp4_scales(part, queue):
             start, width = fp4_ranges[part]
             for r in range(4):
-                nc.sync.dma_start(
+                queue.dma_start(
                     out=fp4_planes[part][:].bitcast(I32)[r:P:32, :, :],
                     in_=fp4_scale_rows[r][:, :, start // 4 : (start + width) // 4],
                 )
@@ -106,9 +107,12 @@ def tile_outlier_split_swiglu_s1_kernel(tc, x, wo_words, wo_scales, wr_words, wr
             offset = col - fp4_ranges[part][0]
             return fp4_planes[part][:, g - 1, offset : offset + width]
 
-        def load_fp8_scales():
+        def load_fp8_scales(half):
             for r in range(4):
-                nc.sync.dma_start(out=fp8_plane[:].bitcast(I32)[FP8_PLANE_ROW + r : P : 32, :], in_=fp8_scale_rows[r])
+                nc.gpsimd.dma_start(
+                    out=fp8_planes[half][:].bitcast(I32)[FP8_PLANE_ROW + r : P : 32, :],
+                    in_=fp8_scale_rows[r][:, half * (F // 4) : (half + 1) * (F // 4)],
+                )
 
         fp4_codes = {}
         fp8_codes = {}
@@ -129,18 +133,19 @@ def tile_outlier_split_swiglu_s1_kernel(tc, x, wo_words, wo_scales, wr_words, wr
             nc.sync.dma_start(out=t[:], in_=x[i * P : (i + 1) * P, :])
             x_tiles[i] = t
 
+        bias_cols = keep.tile([P, N // P], BF16, name="bias_cols", align_bytes=64)
+        nc.gpsimd.dma_start(out=bias_cols[:], in_=bias.rearrange("(p c) -> p c", p=P))
         load_x(0)
         load_x(1)
-        bias_cols = keep.tile([P, 2, 8], BF16, name="bias_cols", align_bytes=64)
-        nc.sync.dma_start(out=bias_cols[:], in_=bias.rearrange("(h p c) -> p h c", h=2, p=P))
-        load_fp4_scales(0)
+        load_fp4_scales(0, nc.sync)
         load_weights(GATE, 0)
-        load_fp8_scales()
+        load_fp8_scales(GATE)
         load_x(2)
-        load_fp4_scales(1)
+        load_fp4_scales(1, nc.sync)
         load_weights(GATE, 1)
         load_x(3)
-        load_fp4_scales(2)
+        load_fp4_scales(2, nc.gpsimd)
+        load_fp8_scales(UP)
         load_weights(UP, 0)
         load_weights(UP, 1)
         for i in range(4, TILES):
@@ -160,48 +165,44 @@ def tile_outlier_split_swiglu_s1_kernel(tc, x, wo_words, wo_scales, wr_words, wr
                     stop=True,
                 )
 
-        bias_rows = {}
+        bias_row = keep.tile([P, N], BF16, name="bias_row", align_bytes=64)
 
-        def turn_bias(half):
+        def turn_bias(part):
             bank = psum.tile([P, 4, P], F32, tag="turn", name="bias_bank")
             for c in range(4):
+                word = 4 * part + c
                 nc.tensor.transpose(
-                    bank[:, c, :], bias_cols[:, half, :].bitcast(F32)[:, c : c + 1].to_broadcast([P, P]), ident[:]
+                    bank[:, c, :], bias_cols[:].bitcast(F32)[:, word : word + 1].to_broadcast([P, P]), ident[:]
                 )
             return bank
 
-        def copy_bias(half, bank):
-            row = keep.tile([P, F], BF16, name="bias_row%d" % half, align_bytes=64)
+        def copy_bias(part, bank):
             nc.scalar.copy(
-                out=row[:].bitcast(F32).rearrange("p (k c) -> p k c", c=4),
+                out=bias_row[:].bitcast(F32).rearrange("p (k c) -> p k c", c=8)[:, :, 4 * part : 4 * part + 4],
                 in_=bank[:].rearrange("p c k -> p k c"),
             )
-            bias_rows[half] = row
 
         sorted_words = {}
 
         def sort_words(i):
-            t = work.tile([P, 4, 2, P], F32, tag="sorted", name="sorted", bufs=3, align_bytes=64)
-            src = x_tiles[i][:].bitcast(F32).rearrange("m (g p u) -> m g u p", g=4, u=2)
-            if i < 3:
-                nc.vector.tensor_copy(out=t[:], in_=src)
-            else:
-                nc.scalar.copy(out=t[:], in_=src)
-            sorted_words[i] = t
+            words = x_tiles[i][:].bitcast(F32).rearrange("m (g p u) -> m g u p", g=4, u=2)
+            for pair, (ga, gb) in enumerate(PASS_PAIRS):
+                t = work.tile([P, 2, 2, P], F32, tag="sorted", name="sorted", bufs=6, align_bytes=64)
+                if i < 3:
+                    nc.vector.tensor_copy(out=t[:], in_=words[:, ga : gb + 1 : gb - ga, :, :])
+                else:
+                    nc.scalar.copy(out=t[:], in_=words[:, ga : gb + 1 : gb - ga, :, :])
+                sorted_words[(i, pair)] = t
 
         x_codes = {}
         x_scales = {}
 
         def turn_pair(i, pair):
             bank = psum.tile([P, 2, 2, P], F32, tag="turn", name="turn_bank")
-            for a, g in enumerate(PASS_PAIRS[pair]):
+            for a in range(2):
                 for u in range(2):
-                    if i < DIRECT_TILES:
-                        src = x_tiles[i][:].bitcast(F32)[:, 2 * P * g + u : 2 * P * (g + 1) : 2]
-                    else:
-                        src = sorted_words[i][:, g, u, :]
-                    nc.tensor.transpose(bank[:, a, u, :], src, ident[:])
-            grouped = work.tile([P, 2 * 4 * P], BF16, tag="grouped", name="grouped", bufs=4, align_bytes=64)
+                    nc.tensor.transpose(bank[:, a, u, :], sorted_words[(i, pair)][:, a, u, :], ident[:])
+            grouped = work.tile([P, 2 * 4 * P], BF16, tag="grouped", name="grouped", bufs=6, align_bytes=64)
             nc.scalar.copy(
                 out=grouped[:].bitcast(F32).rearrange("p (a m u) -> p a m u", a=2, u=2),
                 in_=bank[:].rearrange("p a u m -> p a m u"),
@@ -226,7 +227,7 @@ def tile_outlier_split_swiglu_s1_kernel(tc, x, wo_words, wo_scales, wr_words, wr
             col = half * F + j * COLS + first
             if g == 0:
                 rhs = fp8_codes[(half, j)][:, 4 * first : 4 * (first + width)].bitcast(FP8X4)
-                rhs_scale = fp8_plane[FP8_PLANE_ROW:P, col : col + width]
+                rhs_scale = fp8_planes[half][FP8_PLANE_ROW:P, col - half * F : col - half * F + width]
             else:
                 rhs = fp4_codes[(half, j)][:, g - 1, 2 * first : 2 * (first + width)].bitcast(FP4X4)
                 rhs_scale = fp4_scales(g, col, width)
@@ -242,8 +243,8 @@ def tile_outlier_split_swiglu_s1_kernel(tc, x, wo_words, wo_scales, wr_words, wr
 
         def add_bias(acc, half, block, first, width):
             biased = work.tile([P, COLS], F32, tag="biased%d" % half, name="biased", bufs=5)
-            col = block[1] * COLS + first
-            nc.vector.tensor_tensor(out=biased[:, 0:width], in0=acc, in1=bias_rows[half][:, col : col + width], op=ADD)
+            col = half * F + block[1] * COLS + first
+            nc.vector.tensor_tensor(out=biased[:, 0:width], in0=acc, in1=bias_row[:, col : col + width], op=ADD)
             return biased
 
         activated = {}
@@ -289,10 +290,18 @@ def tile_outlier_split_swiglu_s1_kernel(tc, x, wo_words, wo_scales, wr_words, wr
         sort_words(3)
 
         waiting = None
+        pending = []
         for half, block in order[2:-1]:
             acc = psum.tile([P, COLS], F32, tag="acc", name="acc")
             for g in PASS_ORDER:
                 mx_pass(acc[:], half, block, g, 0, COLS)
+            if block == order[-1][1]:
+                s = work.tile([P, COLS], F32, tag="silu", name="silu", bufs=LEAD + 3)
+                for first, width in TAIL_PIECES:
+                    biased = add_bias(acc[:, first : first + width], half, block, first, width)
+                    nc.scalar.activation(out=s[:, first : first + width], in_=biased[:, 0:width], func=SILU)
+                activated[block] = s
+                continue
             biased = add_bias(acc[:], half, block, 0, COLS)
             if waiting is not None:
                 finish(*waiting)
@@ -303,12 +312,13 @@ def tile_outlier_split_swiglu_s1_kernel(tc, x, wo_words, wo_scales, wr_words, wr
                 waiting = (block, biased, 0, COLS)
             else:
                 for tile in TURN_AFTER.get(block, ()):
-                    turned = [turn_pair(i, pair) for i in tile for pair in range(2)]
-                    for n, grouped in enumerate(turned):
-                        quantize_pair(tile[n // 2], n % 2, grouped)
+                    pending.extend([(i, pair, turn_pair(i, pair)) for i in tile for pair in range(2)])
                 activate(block, biased)
                 for i in SORT_AFTER.get(block, ()):
                     sort_words(i)
+            for job in pending[:2]:
+                quantize_pair(*job)
+            pending = pending[2:]
         if waiting is not None:
             finish(*waiting)
             waiting = None

@@ -18,20 +18,23 @@ MULT = mybir.AluOpType.mult
 SILU = mybir.ActivationFunctionType.Silu
 
 P = 128
-COLS = 512
-NARROW = 128
 TILES = M // P
+COLS = 512
 GATE, UP = 0, 1
+FP4_PASSES = 3
 PASS_PAIRS = ((1, 2), (0, 3))
 PASS_ORDER = (1, 2, 3, 0)
 FP8_PLANE_ROW = 4
+BIAS_WORDS = N // 2 // P
+WORDS_PER_BANK = 4
+
 LEAD = 6
-MIN_LEAD = 0
-DIRECT_TILES = 0
-WARM_RUNS = (13, 8, 0, 0)
-TURN_AFTER = {(2, 0): [(3,)], (3, 1): [(4, 5)], (5, 1): [(6, 7)]}
-SORT_AFTER = {(2, 1): [4], (3, 0): [5], (4, 1): [6], (5, 0): [7]}
-TAIL_PIECES = [(0, 256), (256, 256)]
+VECTOR_SORTED_TILES = 3
+TRANSPOSE_RUNS = ((3,), (4, 5), (6, 7))
+PAIRS_PER_STEP = 2
+TAIL_COLS = COLS // 2
+NARROW = 128
+WARM_PASSES = 13
 
 
 def block_order():
@@ -43,19 +46,27 @@ def block_order():
 
 def group_order():
     blocks = block_order()
-    order = [(GATE, b) for b in blocks[:LEAD]]
-    gates = LEAD
+    order = [(GATE, block) for block in blocks[:LEAD]]
     ups = 0
-    while ups < len(blocks):
-        order.append((UP, blocks[ups]))
-        ups = ups + 1
-        if gates - ups > MIN_LEAD and ups < len(blocks) and (gates % 2 == 0 or gates - ups > len(blocks) - gates):
-            order.append((UP, blocks[ups]))
-            ups = ups + 1
-        if gates < len(blocks):
-            order.append((GATE, blocks[gates]))
-            gates = gates + 1
+    for gates in range(LEAD, len(blocks)):
+        count = 2 if (gates - LEAD) % 2 == 0 else 1
+        order.extend([(UP, block) for block in blocks[ups : ups + count]])
+        ups = ups + count
+        order.append((GATE, blocks[gates]))
+    order.extend([(UP, block) for block in blocks[ups:]])
     return order
+
+
+def preparation_order():
+    blocks = block_order()
+    transpose_after = {}
+    sort_after = {}
+    for run in TRANSPOSE_RUNS:
+        place = blocks.index((run[0], 0)) - 1
+        transpose_after[blocks[place]] = run
+        for n, i in enumerate(run):
+            sort_after[blocks[place - 2 + n]] = i
+    return transpose_after, sort_after
 
 
 def tile_outlier_split_swiglu_s1_kernel(tc, x, wo_words, wo_scales, wr_words, wr_scales, bias, out):
@@ -77,39 +88,37 @@ def tile_outlier_split_swiglu_s1_kernel(tc, x, wo_words, wo_scales, wr_words, wr
         make_identity(nc, ident[:])
 
         fp4_ranges = [(0, COLS), (COLS, COLS), (F, F)]
-        fp4_planes = []
-        for start, width in fp4_ranges:
-            plane = keep.tile([P, 3, width], U8, name="fp4_plane%d" % start, align_bytes=64)
-            fp4_planes.append(plane)
+        fp4_planes = [
+            keep.tile([P, FP4_PASSES, width], U8, name="fp4_plane%d" % start, align_bytes=64)
+            for start, width in fp4_ranges
+        ]
         fp8_planes = [keep.tile([P, F], U8, name="fp8_plane%d" % half, align_bytes=64) for half in (GATE, UP)]
         nc.vector.memset(fp4_planes[0][:].bitcast(I32), 0)
         nc.vector.quantize_mx(out=warm_codes[:].bitcast(FP8X4), scales=warm_scales[:], in_=warm_in[:])
-        nc.vector.memset(fp8_planes[GATE][:].bitcast(I32), 0)
-        nc.vector.memset(fp4_planes[1][:].bitcast(I32), 0)
-        nc.vector.memset(fp4_planes[2][:].bitcast(I32), 0)
-        nc.vector.memset(fp8_planes[UP][:].bitcast(I32), 0)
+        for plane in (fp8_planes[GATE], fp4_planes[1], fp4_planes[2], fp8_planes[UP]):
+            nc.vector.memset(plane[:].bitcast(I32), 0)
 
         fp4_scale_rows = wr_scales.bitcast(I32).rearrange("g (q r) w -> r q g w", r=4)
         fp8_scale_rows = wo_scales[0].bitcast(I32).rearrange("(q r) w -> r q w", r=4)
         fp4_rows = wr_words.bitcast(I32).rearrange("g p w -> p g w")
         fp8_rows = wo_words[0].rearrange("p n t -> p (n t)").bitcast(I32)
 
-        def load_fp4_scales(part, queue):
+        def load_fp4_scales(part):
             start, width = fp4_ranges[part]
             for r in range(4):
-                queue.dma_start(
+                nc.sync.dma_start(
                     out=fp4_planes[part][:].bitcast(I32)[r:P:32, :, :],
                     in_=fp4_scale_rows[r][:, :, start // 4 : (start + width) // 4],
                 )
 
         def fp4_scales(g, col, width):
-            part = min(col // COLS, 2)
+            part = min(col // COLS, len(fp4_ranges) - 1)
             offset = col - fp4_ranges[part][0]
             return fp4_planes[part][:, g - 1, offset : offset + width]
 
         def load_fp8_scales(half):
             for r in range(4):
-                nc.gpsimd.dma_start(
+                nc.sync.dma_start(
                     out=fp8_planes[half][:].bitcast(I32)[FP8_PLANE_ROW + r : P : 32, :],
                     in_=fp8_scale_rows[r][:, half * (F // 4) : (half + 1) * (F // 4)],
                 )
@@ -119,66 +128,53 @@ def tile_outlier_split_swiglu_s1_kernel(tc, x, wo_words, wo_scales, wr_words, wr
 
         def load_weights(half, j):
             col = half * F + j * COLS
-            c4 = keep.tile([P, 3, 2 * COLS], U8, name="fp4_codes%d%d" % (half, j), align_bytes=64)
-            nc.sync.dma_start(out=c4[:].bitcast(I32), in_=fp4_rows[:, :, col // 2 : (col + COLS) // 2])
-            c8 = keep.tile([P, 4 * COLS], U8, name="fp8_codes%d%d" % (half, j), align_bytes=64)
-            nc.sync.dma_start(out=c8[:].bitcast(I32), in_=fp8_rows[:, col : col + COLS])
-            fp4_codes[(half, j)] = c4
-            fp8_codes[(half, j)] = c8
+            codes4 = keep.tile([P, FP4_PASSES, 2 * COLS], U8, name="fp4_codes%d%d" % (half, j), align_bytes=64)
+            nc.sync.dma_start(out=codes4[:].bitcast(I32), in_=fp4_rows[:, :, col // 2 : (col + COLS) // 2])
+            codes8 = keep.tile([P, 4 * COLS], U8, name="fp8_codes%d%d" % (half, j), align_bytes=64)
+            nc.sync.dma_start(out=codes8[:].bitcast(I32), in_=fp8_rows[:, col : col + COLS])
+            fp4_codes[(half, j)] = codes4
+            fp8_codes[(half, j)] = codes8
 
         x_tiles = {}
 
         def load_x(i):
-            t = keep.tile([P, K], BF16, name="x%d" % i, align_bytes=64)
-            nc.sync.dma_start(out=t[:], in_=x[i * P : (i + 1) * P, :])
-            x_tiles[i] = t
+            x_tile = keep.tile([P, K], BF16, name="x%d" % i, align_bytes=64)
+            nc.sync.dma_start(out=x_tile[:], in_=x[i * P : (i + 1) * P, :])
+            x_tiles[i] = x_tile
 
         bias_cols = keep.tile([P, N // P], BF16, name="bias_cols", align_bytes=64)
-        nc.gpsimd.dma_start(out=bias_cols[:], in_=bias.rearrange("(p c) -> p c", p=P))
+        nc.sync.dma_start(out=bias_cols[:], in_=bias.rearrange("(p c) -> p c", p=P))
         load_x(0)
         load_x(1)
-        load_fp4_scales(0, nc.sync)
+        load_fp4_scales(0)
         load_weights(GATE, 0)
         load_fp8_scales(GATE)
         load_x(2)
-        load_fp4_scales(1, nc.sync)
+        load_fp4_scales(1)
         load_weights(GATE, 1)
         load_x(3)
-        load_fp4_scales(2, nc.gpsimd)
+        load_fp4_scales(2)
         load_fp8_scales(UP)
         load_weights(UP, 0)
         load_weights(UP, 1)
         for i in range(4, TILES):
             load_x(i)
 
-        warm_bank = psum.tile([P, P], F32, tag="acc", name="warm_bank")
-
-        def warm(count):
-            for step in range(count):
-                nc.tensor.matmul_mx(
-                    out=warm_bank[:],
-                    lhsT=warm_codes[:].bitcast(FP8X4),
-                    lhsT_scale=warm_scales[:],
-                    rhs=warm_codes[:].bitcast(FP8X4),
-                    rhs_scale=warm_scales[:],
-                    start=True,
-                    stop=True,
-                )
-
         bias_row = keep.tile([P, N], BF16, name="bias_row", align_bytes=64)
 
-        def turn_bias(part):
-            bank = psum.tile([P, 4, P], F32, tag="turn", name="bias_bank")
-            for c in range(4):
-                word = 4 * part + c
-                nc.tensor.transpose(
-                    bank[:, c, :], bias_cols[:].bitcast(F32)[:, word : word + 1].to_broadcast([P, P]), ident[:]
-                )
+        def transpose_bias(part):
+            bank = psum.tile([P, WORDS_PER_BANK, P], F32, tag="turn", name="bias_bank")
+            for c in range(WORDS_PER_BANK):
+                word = WORDS_PER_BANK * part + c
+                column = bias_cols[:].bitcast(F32)[:, word : word + 1]
+                nc.tensor.transpose(bank[:, c, :], column.to_broadcast([P, P]), ident[:])
             return bank
 
         def copy_bias(part, bank):
+            first_word = WORDS_PER_BANK * part
+            by_source = bias_row[:].bitcast(F32).rearrange("p (k c) -> p k c", c=BIAS_WORDS)
             nc.scalar.copy(
-                out=bias_row[:].bitcast(F32).rearrange("p (k c) -> p k c", c=8)[:, :, 4 * part : 4 * part + 4],
+                out=by_source[:, :, first_word : first_word + WORDS_PER_BANK],
                 in_=bank[:].rearrange("p c k -> p k c"),
             )
 
@@ -186,18 +182,16 @@ def tile_outlier_split_swiglu_s1_kernel(tc, x, wo_words, wo_scales, wr_words, wr
 
         def sort_words(i):
             words = x_tiles[i][:].bitcast(F32).rearrange("m (g p u) -> m g u p", g=4, u=2)
-            for pair, (ga, gb) in enumerate(PASS_PAIRS):
-                t = work.tile([P, 2, 2, P], F32, tag="sorted", name="sorted", bufs=6, align_bytes=64)
-                if i < 3:
-                    nc.vector.tensor_copy(out=t[:], in_=words[:, ga : gb + 1 : gb - ga, :, :])
+            for pair, (g_first, g_second) in enumerate(PASS_PAIRS):
+                source = words[:, g_first : g_second + 1 : g_second - g_first, :, :]
+                by_slot = work.tile([P, 2, 2, P], F32, tag="sorted", name="sorted", bufs=6, align_bytes=64)
+                if i < VECTOR_SORTED_TILES:
+                    nc.vector.tensor_copy(out=by_slot[:], in_=source)
                 else:
-                    nc.scalar.copy(out=t[:], in_=words[:, ga : gb + 1 : gb - ga, :, :])
-                sorted_words[(i, pair)] = t
+                    nc.scalar.copy(out=by_slot[:], in_=source)
+                sorted_words[(i, pair)] = by_slot
 
-        x_codes = {}
-        x_scales = {}
-
-        def turn_pair(i, pair):
+        def transpose_pair(i, pair):
             bank = psum.tile([P, 2, 2, P], F32, tag="turn", name="turn_bank")
             for a in range(2):
                 for u in range(2):
@@ -207,7 +201,13 @@ def tile_outlier_split_swiglu_s1_kernel(tc, x, wo_words, wo_scales, wr_words, wr
                 out=grouped[:].bitcast(F32).rearrange("p (a m u) -> p a m u", a=2, u=2),
                 in_=bank[:].rearrange("p a u m -> p a m u"),
             )
-            return grouped
+            return (i, pair, grouped)
+
+        def transpose_tile(i):
+            return [transpose_pair(i, pair) for pair in range(len(PASS_PAIRS))]
+
+        x_codes = {}
+        x_scales = {}
 
         def quantize_pair(i, pair, grouped):
             codes = keep.tile([P, 2 * P], U32, name="x_codes%d_%d" % (i, pair), align_bytes=64)
@@ -217,20 +217,15 @@ def tile_outlier_split_swiglu_s1_kernel(tc, x, wo_words, wo_scales, wr_words, wr
                 x_codes[(i, g)] = codes[:, a * P : (a + 1) * P]
                 x_scales[(i, g)] = scales[:, a * P : (a + 1) * P]
 
-        def prepare_tile(i):
-            turned = [turn_pair(i, pair) for pair in range(2)]
-            for pair in range(2):
-                quantize_pair(i, pair, turned[pair])
-
         def mx_pass(acc, half, block, g, first, width):
             i, j = block
-            col = half * F + j * COLS + first
+            col_in_half = j * COLS + first
             if g == 0:
                 rhs = fp8_codes[(half, j)][:, 4 * first : 4 * (first + width)].bitcast(FP8X4)
-                rhs_scale = fp8_planes[half][FP8_PLANE_ROW:P, col - half * F : col - half * F + width]
+                rhs_scale = fp8_planes[half][FP8_PLANE_ROW:P, col_in_half : col_in_half + width]
             else:
                 rhs = fp4_codes[(half, j)][:, g - 1, 2 * first : 2 * (first + width)].bitcast(FP4X4)
-                rhs_scale = fp4_scales(g, col, width)
+                rhs_scale = fp4_scales(g, half * F + col_in_half, width)
             nc.tensor.matmul_mx(
                 out=acc,
                 lhsT=x_codes[(i, g)].bitcast(FP8X4),
@@ -241,6 +236,12 @@ def tile_outlier_split_swiglu_s1_kernel(tc, x, wo_words, wo_scales, wr_words, wr
                 stop=(g == PASS_ORDER[-1]),
             )
 
+        def multiply(half, block):
+            acc = psum.tile([P, COLS], F32, tag="acc", name="acc")
+            for g in PASS_ORDER:
+                mx_pass(acc[:], half, block, g, 0, COLS)
+            return acc
+
         def add_bias(acc, half, block, first, width):
             biased = work.tile([P, COLS], F32, tag="biased%d" % half, name="biased", bufs=5)
             col = half * F + block[1] * COLS + first
@@ -249,10 +250,10 @@ def tile_outlier_split_swiglu_s1_kernel(tc, x, wo_words, wo_scales, wr_words, wr
 
         activated = {}
 
-        def activate(block, biased):
-            s = work.tile([P, COLS], F32, tag="silu", name="silu", bufs=LEAD + 3)
-            nc.scalar.activation(out=s[:], in_=biased[:], func=SILU)
-            activated[block] = s
+        def new_silu_tile(block):
+            silu = work.tile([P, COLS], F32, tag="silu", name="silu", bufs=LEAD + 3)
+            activated[block] = silu
+            return silu
 
         def finish(block, biased, first, width):
             i, j = block
@@ -264,74 +265,79 @@ def tile_outlier_split_swiglu_s1_kernel(tc, x, wo_words, wo_scales, wr_words, wr
             nc.sync.dma_start(out=out[i * P : (i + 1) * P, col : col + width], in_=result[:])
 
         order = group_order()
+        transpose_after, sort_after = preparation_order()
 
         sort_words(0)
         sort_words(1)
-        warm(WARM_RUNS[0])
-        turned = [turn_pair(0, pair) for pair in range(2)]
-        bias_banks = [turn_bias(half) for half in (GATE, UP)]
-        turned.extend([turn_pair(1, pair) for pair in range(2)])
-        for half in (GATE, UP):
-            copy_bias(half, bias_banks[half])
-        for n, grouped in enumerate(turned):
-            quantize_pair(n // 2, n % 2, grouped)
+        warm_bank = psum.tile([P, P], F32, tag="acc", name="warm_bank")
+        for step in range(WARM_PASSES):
+            nc.tensor.matmul_mx(
+                out=warm_bank[:],
+                lhsT=warm_codes[:].bitcast(FP8X4),
+                lhsT_scale=warm_scales[:],
+                rhs=warm_codes[:].bitcast(FP8X4),
+                rhs_scale=warm_scales[:],
+                start=True,
+                stop=True,
+            )
+        turned = transpose_tile(0)
+        bias_banks = [transpose_bias(part) for part in range(BIAS_WORDS // WORDS_PER_BANK)]
+        turned.extend(transpose_tile(1))
+        for part, bank in enumerate(bias_banks):
+            copy_bias(part, bank)
+        for job in turned:
+            quantize_pair(*job)
         sort_words(2)
 
-        first_blocks = [order[0][1], order[1][1]]
+        first_blocks = [block for half, block in order[:2]]
         first_accs = [psum.tile([P, COLS], F32, tag="acc", name="acc") for block in first_blocks]
         for passes in (PASS_ORDER[:-1], PASS_ORDER[-1:]):
             for acc, block in zip(first_accs, first_blocks):
                 for g in passes:
                     mx_pass(acc[:], GATE, block, g, 0, COLS)
         first_biased = [add_bias(acc[:], GATE, block, 0, COLS) for acc, block in zip(first_accs, first_blocks)]
-        prepare_tile(2)
+        for job in transpose_tile(2):
+            quantize_pair(*job)
         for block, biased in zip(first_blocks, first_biased):
-            activate(block, biased)
-        sort_words(3)
+            nc.scalar.activation(out=new_silu_tile(block)[:], in_=biased[:], func=SILU)
 
-        waiting = None
-        pending = []
-        for half, block in order[2:-1]:
-            acc = psum.tile([P, COLS], F32, tag="acc", name="acc")
-            for g in PASS_ORDER:
-                mx_pass(acc[:], half, block, g, 0, COLS)
-            if block == order[-1][1]:
-                s = work.tile([P, COLS], F32, tag="silu", name="silu", bufs=LEAD + 3)
-                for first, width in TAIL_PIECES:
-                    biased = add_bias(acc[:, first : first + width], half, block, first, width)
-                    nc.scalar.activation(out=s[:, first : first + width], in_=biased[:, 0:width], func=SILU)
-                activated[block] = s
-                continue
+        unfinished = []
+        unquantized = []
+        for half, block in order[2:-3]:
+            acc = multiply(half, block)
             biased = add_bias(acc[:], half, block, 0, COLS)
-            if waiting is not None:
-                finish(*waiting)
-                waiting = None
-            if half == UP and block == (TILES - 1, 0):
-                finish(block, biased, 0, COLS)
-            elif half == UP:
-                waiting = (block, biased, 0, COLS)
+            for job in unfinished:
+                finish(*job)
+            unfinished = []
+            if half == UP:
+                unfinished = [(block, biased, 0, COLS)]
             else:
-                for tile in TURN_AFTER.get(block, ()):
-                    pending.extend([(i, pair, turn_pair(i, pair)) for i in tile for pair in range(2)])
-                activate(block, biased)
-                for i in SORT_AFTER.get(block, ()):
-                    sort_words(i)
-            for job in pending[:2]:
+                for i in transpose_after.get(block, ()):
+                    unquantized.extend(transpose_tile(i))
+                if block in sort_after:
+                    sort_words(sort_after[block])
+                nc.scalar.activation(out=new_silu_tile(block)[:], in_=biased[:], func=SILU)
+            for job in unquantized[:PAIRS_PER_STEP]:
                 quantize_pair(*job)
-            pending = pending[2:]
-        if waiting is not None:
-            finish(*waiting)
-            waiting = None
+            unquantized = unquantized[PAIRS_PER_STEP:]
+
+        block = order[-3][1]
+        acc = multiply(UP, block)
+        finish(block, add_bias(acc[:], UP, block, 0, COLS), 0, COLS)
 
         block = order[-1][1]
-        for first, width in TAIL_PIECES:
+        acc = multiply(GATE, block)
+        silu = new_silu_tile(block)
+        for first in range(0, COLS, TAIL_COLS):
+            biased = add_bias(acc[:, first : first + TAIL_COLS], GATE, block, first, TAIL_COLS)
+            nc.scalar.activation(out=silu[:, first : first + TAIL_COLS], in_=biased[:, 0:TAIL_COLS], func=SILU)
+
+        halves = []
+        for first in range(0, COLS, TAIL_COLS):
             acc = psum.tile([P, COLS], F32, tag="turn", name="tail_acc")
-            step = NARROW if width < COLS else COLS
-            for sub in range(0, width, step):
+            for sub in range(0, TAIL_COLS, NARROW):
                 for g in PASS_ORDER:
-                    mx_pass(acc[:, sub : sub + step], UP, block, g, first + sub, step)
-            biased = add_bias(acc[:, 0:width], UP, block, first, width)
-            if waiting is not None:
-                finish(*waiting)
-            waiting = (block, biased, first, width)
-        finish(*waiting)
+                    mx_pass(acc[:, sub : sub + NARROW], UP, block, g, first + sub, NARROW)
+            halves.append((block, add_bias(acc[:, 0:TAIL_COLS], UP, block, first, TAIL_COLS), first, TAIL_COLS))
+        for job in halves:
+            finish(*job)

from contextlib import ExitStack

import concourse.mybir as mybir
from concourse.masks import make_identity

M, K, N, F = 1024, 2048, 2048, 1024
FLOPS = 2 * M * K * N

F32 = mybir.dt.float32
BF16 = mybir.dt.bfloat16
I32 = mybir.dt.int32
U32 = mybir.dt.uint32
U8 = mybir.dt.uint8
FP8X4 = mybir.dt.float8_e4m3fn_x4
FP4X4 = mybir.dt.float4_e2m1fn_x4
ADD = mybir.AluOpType.add
MULT = mybir.AluOpType.mult
SILU = mybir.ActivationFunctionType.Silu

P = 128
TILES = M // P
COLS = 512
GATE, UP = 0, 1
FP4_PASSES = 3
PASS_PAIRS = ((1, 2), (0, 3))
PASS_ORDER = (1, 2, 3, 0)
FP8_PLANE_ROW = 4
BIAS_WORDS = N // 2 // P
WORDS_PER_BANK = 4

LEAD = 6
VECTOR_SORTED_TILES = 3
TRANSPOSE_RUNS = ((3,), (4, 5), (6, 7))
PAIRS_PER_STEP = 2
TAIL_COLS = COLS // 2
NARROW = 128
WARM_PASSES = 13


def block_order():
    blocks = [(0, 0), (1, 0), (0, 1), (1, 1)]
    for i in range(2, TILES):
        blocks.extend([(i, 0), (i, 1)])
    return blocks


def group_order():
    blocks = block_order()
    order = [(GATE, block) for block in blocks[:LEAD]]
    ups = 0
    for gates in range(LEAD, len(blocks)):
        count = 2 if (gates - LEAD) % 2 == 0 else 1
        order.extend([(UP, block) for block in blocks[ups : ups + count]])
        ups = ups + count
        order.append((GATE, blocks[gates]))
    order.extend([(UP, block) for block in blocks[ups:]])
    return order


def preparation_order():
    blocks = block_order()
    transpose_after = {}
    sort_after = {}
    for run in TRANSPOSE_RUNS:
        place = blocks.index((run[0], 0)) - 1
        transpose_after[blocks[place]] = run
        for n, i in enumerate(run):
            sort_after[blocks[place - 2 + n]] = i
    return transpose_after, sort_after


def tile_outlier_split_swiglu_s1_kernel(tc, x, wo_words, wo_scales, wr_words, wr_scales, bias, out):
    nc = tc.nc
    with ExitStack() as ctx:
        keep = ctx.enter_context(tc.tile_pool(name="keep", bufs=1))
        work = ctx.enter_context(tc.tile_pool(name="work", bufs=3))
        psum = ctx.enter_context(tc.psum_pool(name="psum", bufs=4))
        ctx.enter_context(tc.manual_schedule())

        warm_in = keep.tile([P, 4 * P], BF16, name="warm_in", align_bytes=64)
        warm_codes = keep.tile([P, P], U32, name="warm_codes", align_bytes=64)
        warm_scales = keep.tile([P, P], U8, name="warm_scales", align_bytes=64)
        warm_silu = keep.tile([P, 1], F32, name="warm_silu")
        nc.vector.memset(warm_in[:], 1.0)
        nc.scalar.activation(out=warm_silu[:], in_=warm_in[:, 0:1], func=SILU)

        ident = keep.tile([P, P], F32, name="ident")
        make_identity(nc, ident[:])

        fp4_ranges = [(0, COLS), (COLS, COLS), (F, F)]
        fp4_planes = [
            keep.tile([P, FP4_PASSES, width], U8, name="fp4_plane%d" % start, align_bytes=64)
            for start, width in fp4_ranges
        ]
        fp8_planes = [keep.tile([P, F], U8, name="fp8_plane%d" % half, align_bytes=64) for half in (GATE, UP)]
        nc.vector.memset(fp4_planes[0][:].bitcast(I32), 0)
        nc.vector.quantize_mx(out=warm_codes[:].bitcast(FP8X4), scales=warm_scales[:], in_=warm_in[:])
        for plane in (fp8_planes[GATE], fp4_planes[1], fp4_planes[2], fp8_planes[UP]):
            nc.vector.memset(plane[:].bitcast(I32), 0)

        fp4_scale_rows = wr_scales.bitcast(I32).rearrange("g (q r) w -> r q g w", r=4)
        fp8_scale_rows = wo_scales[0].bitcast(I32).rearrange("(q r) w -> r q w", r=4)
        fp4_rows = wr_words.bitcast(I32).rearrange("g p w -> p g w")
        fp8_rows = wo_words[0].rearrange("p n t -> p (n t)").bitcast(I32)

        def load_fp4_scales(part):
            start, width = fp4_ranges[part]
            for r in range(4):
                nc.sync.dma_start(
                    out=fp4_planes[part][:].bitcast(I32)[r:P:32, :, :],
                    in_=fp4_scale_rows[r][:, :, start // 4 : (start + width) // 4],
                )

        def fp4_scales(g, col, width):
            part = min(col // COLS, len(fp4_ranges) - 1)
            offset = col - fp4_ranges[part][0]
            return fp4_planes[part][:, g - 1, offset : offset + width]

        def load_fp8_scales(half):
            for r in range(4):
                nc.sync.dma_start(
                    out=fp8_planes[half][:].bitcast(I32)[FP8_PLANE_ROW + r : P : 32, :],
                    in_=fp8_scale_rows[r][:, half * (F // 4) : (half + 1) * (F // 4)],
                )

        fp4_codes = {}
        fp8_codes = {}

        def load_weights(half, j):
            col = half * F + j * COLS
            codes4 = keep.tile([P, FP4_PASSES, 2 * COLS], U8, name="fp4_codes%d%d" % (half, j), align_bytes=64)
            nc.sync.dma_start(out=codes4[:].bitcast(I32), in_=fp4_rows[:, :, col // 2 : (col + COLS) // 2])
            codes8 = keep.tile([P, 4 * COLS], U8, name="fp8_codes%d%d" % (half, j), align_bytes=64)
            nc.sync.dma_start(out=codes8[:].bitcast(I32), in_=fp8_rows[:, col : col + COLS])
            fp4_codes[(half, j)] = codes4
            fp8_codes[(half, j)] = codes8

        x_tiles = {}

        def load_x(i):
            x_tile = keep.tile([P, K], BF16, name="x%d" % i, align_bytes=64)
            nc.sync.dma_start(out=x_tile[:], in_=x[i * P : (i + 1) * P, :])
            x_tiles[i] = x_tile

        bias_cols = keep.tile([P, N // P], BF16, name="bias_cols", align_bytes=64)
        nc.sync.dma_start(out=bias_cols[:], in_=bias.rearrange("(p c) -> p c", p=P))
        load_x(0)
        load_x(1)
        load_fp4_scales(0)
        load_weights(GATE, 0)
        load_fp8_scales(GATE)
        load_x(2)
        load_fp4_scales(1)
        load_weights(GATE, 1)
        load_x(3)
        load_fp4_scales(2)
        load_fp8_scales(UP)
        load_weights(UP, 0)
        load_weights(UP, 1)
        for i in range(4, TILES):
            load_x(i)

        bias_row = keep.tile([P, N], BF16, name="bias_row", align_bytes=64)

        def transpose_bias(part):
            bank = psum.tile([P, WORDS_PER_BANK, P], F32, tag="turn", name="bias_bank")
            for c in range(WORDS_PER_BANK):
                word = WORDS_PER_BANK * part + c
                column = bias_cols[:].bitcast(F32)[:, word : word + 1]
                nc.tensor.transpose(bank[:, c, :], column.to_broadcast([P, P]), ident[:])
            return bank

        def copy_bias(part, bank):
            first_word = WORDS_PER_BANK * part
            by_source = bias_row[:].bitcast(F32).rearrange("p (k c) -> p k c", c=BIAS_WORDS)
            nc.scalar.copy(
                out=by_source[:, :, first_word : first_word + WORDS_PER_BANK],
                in_=bank[:].rearrange("p c k -> p k c"),
            )

        sorted_words = {}

        def sort_words(i):
            words = x_tiles[i][:].bitcast(F32).rearrange("m (g p u) -> m g u p", g=4, u=2)
            for pair, (g_first, g_second) in enumerate(PASS_PAIRS):
                source = words[:, g_first : g_second + 1 : g_second - g_first, :, :]
                by_slot = work.tile([P, 2, 2, P], F32, tag="sorted", name="sorted", bufs=6, align_bytes=64)
                if i < VECTOR_SORTED_TILES:
                    nc.vector.tensor_copy(out=by_slot[:], in_=source)
                else:
                    nc.scalar.copy(out=by_slot[:], in_=source)
                sorted_words[(i, pair)] = by_slot

        def transpose_pair(i, pair):
            bank = psum.tile([P, 2, 2, P], F32, tag="turn", name="turn_bank")
            for a in range(2):
                for u in range(2):
                    nc.tensor.transpose(bank[:, a, u, :], sorted_words[(i, pair)][:, a, u, :], ident[:])
            grouped = work.tile([P, 2 * 4 * P], BF16, tag="grouped", name="grouped", bufs=6, align_bytes=64)
            nc.scalar.copy(
                out=grouped[:].bitcast(F32).rearrange("p (a m u) -> p a m u", a=2, u=2),
                in_=bank[:].rearrange("p a u m -> p a m u"),
            )
            return (i, pair, grouped)

        def transpose_tile(i):
            return [transpose_pair(i, pair) for pair in range(len(PASS_PAIRS))]

        x_codes = {}
        x_scales = {}

        def quantize_pair(i, pair, grouped):
            codes = keep.tile([P, 2 * P], U32, name="x_codes%d_%d" % (i, pair), align_bytes=64)
            scales = keep.tile([P, 2 * P], U8, name="x_scales%d_%d" % (i, pair), align_bytes=64)
            nc.vector.quantize_mx(out=codes[:].bitcast(FP8X4), scales=scales[:], in_=grouped[:])
            for a, g in enumerate(PASS_PAIRS[pair]):
                x_codes[(i, g)] = codes[:, a * P : (a + 1) * P]
                x_scales[(i, g)] = scales[:, a * P : (a + 1) * P]

        def mx_pass(acc, half, block, g, first, width):
            i, j = block
            col_in_half = j * COLS + first
            if g == 0:
                rhs = fp8_codes[(half, j)][:, 4 * first : 4 * (first + width)].bitcast(FP8X4)
                rhs_scale = fp8_planes[half][FP8_PLANE_ROW:P, col_in_half : col_in_half + width]
            else:
                rhs = fp4_codes[(half, j)][:, g - 1, 2 * first : 2 * (first + width)].bitcast(FP4X4)
                rhs_scale = fp4_scales(g, half * F + col_in_half, width)
            nc.tensor.matmul_mx(
                out=acc,
                lhsT=x_codes[(i, g)].bitcast(FP8X4),
                lhsT_scale=x_scales[(i, g)],
                rhs=rhs,
                rhs_scale=rhs_scale,
                start=(g == PASS_ORDER[0]),
                stop=(g == PASS_ORDER[-1]),
            )

        def multiply(half, block):
            acc = psum.tile([P, COLS], F32, tag="acc", name="acc")
            for g in PASS_ORDER:
                mx_pass(acc[:], half, block, g, 0, COLS)
            return acc

        def add_bias(acc, half, block, first, width):
            biased = work.tile([P, COLS], F32, tag="biased%d" % half, name="biased", bufs=5)
            col = half * F + block[1] * COLS + first
            nc.vector.tensor_tensor(out=biased[:, 0:width], in0=acc, in1=bias_row[:, col : col + width], op=ADD)
            return biased

        activated = {}

        def new_silu_tile(block):
            silu = work.tile([P, COLS], F32, tag="silu", name="silu", bufs=LEAD + 3)
            activated[block] = silu
            return silu

        def finish(block, biased, first, width):
            i, j = block
            result = keep.tile([P, width], F32, name="result%d_%d_%d" % (i, j, first))
            nc.vector.tensor_tensor(
                out=result[:], in0=biased[:, 0:width], in1=activated[block][:, first : first + width], op=MULT
            )
            col = j * COLS + first
            nc.sync.dma_start(out=out[i * P : (i + 1) * P, col : col + width], in_=result[:])

        order = group_order()
        transpose_after, sort_after = preparation_order()

        sort_words(0)
        sort_words(1)
        warm_bank = psum.tile([P, P], F32, tag="acc", name="warm_bank")
        for step in range(WARM_PASSES):
            nc.tensor.matmul_mx(
                out=warm_bank[:],
                lhsT=warm_codes[:].bitcast(FP8X4),
                lhsT_scale=warm_scales[:],
                rhs=warm_codes[:].bitcast(FP8X4),
                rhs_scale=warm_scales[:],
                start=True,
                stop=True,
            )
        turned = transpose_tile(0)
        bias_banks = [transpose_bias(part) for part in range(BIAS_WORDS // WORDS_PER_BANK)]
        turned.extend(transpose_tile(1))
        for part, bank in enumerate(bias_banks):
            copy_bias(part, bank)
        for job in turned:
            quantize_pair(*job)
        sort_words(2)

        first_blocks = [block for half, block in order[:2]]
        first_accs = [psum.tile([P, COLS], F32, tag="acc", name="acc") for block in first_blocks]
        for passes in (PASS_ORDER[:-1], PASS_ORDER[-1:]):
            for acc, block in zip(first_accs, first_blocks):
                for g in passes:
                    mx_pass(acc[:], GATE, block, g, 0, COLS)
        first_biased = [add_bias(acc[:], GATE, block, 0, COLS) for acc, block in zip(first_accs, first_blocks)]
        for job in transpose_tile(2):
            quantize_pair(*job)
        for block, biased in zip(first_blocks, first_biased):
            nc.scalar.activation(out=new_silu_tile(block)[:], in_=biased[:], func=SILU)

        unfinished = []
        unquantized = []
        for half, block in order[2:-3]:
            acc = multiply(half, block)
            biased = add_bias(acc[:], half, block, 0, COLS)
            for job in unfinished:
                finish(*job)
            unfinished = []
            if half == UP:
                unfinished = [(block, biased, 0, COLS)]
            else:
                for i in transpose_after.get(block, ()):
                    unquantized.extend(transpose_tile(i))
                if block in sort_after:
                    sort_words(sort_after[block])
                nc.scalar.activation(out=new_silu_tile(block)[:], in_=biased[:], func=SILU)
            for job in unquantized[:PAIRS_PER_STEP]:
                quantize_pair(*job)
            unquantized = unquantized[PAIRS_PER_STEP:]

        block = order[-3][1]
        acc = multiply(UP, block)
        finish(block, add_bias(acc[:], UP, block, 0, COLS), 0, COLS)

        block = order[-1][1]
        acc = multiply(GATE, block)
        silu = new_silu_tile(block)
        for first in range(0, COLS, TAIL_COLS):
            biased = add_bias(acc[:, first : first + TAIL_COLS], GATE, block, first, TAIL_COLS)
            nc.scalar.activation(out=silu[:, first : first + TAIL_COLS], in_=biased[:, 0:TAIL_COLS], func=SILU)

        halves = []
        for first in range(0, COLS, TAIL_COLS):
            acc = psum.tile([P, COLS], F32, tag="turn", name="tail_acc")
            for sub in range(0, TAIL_COLS, NARROW):
                for g in PASS_ORDER:
                    mx_pass(acc[:, sub : sub + NARROW], UP, block, g, first + sub, NARROW)
            halves.append((block, add_bias(acc[:, 0:TAIL_COLS], UP, block, first, TAIL_COLS), first, TAIL_COLS))
        for job in halves:
            finish(*job)
